import numpy as np
import ml_dtypes


def mxq(x, axis, fmt="e4m3"):
    dtype, down = {"e4m3": (ml_dtypes.float8_e4m3fn, 7), "e5m2": (ml_dtypes.float8_e5m2, 14)}[fmt]
    v = np.moveaxis(np.asarray(x, np.float32).astype(ml_dtypes.bfloat16).astype(np.float64), axis, -1)
    blocks = v.reshape(v.shape[:-1] + (-1, 32))
    amax = np.abs(blocks).max(-1, keepdims=True)
    byte = np.maximum(np.where(amax > 0, np.frexp(amax)[1] - 1 + 127, 0) - down, 1)
    scale = np.exp2(byte - 127.0)
    codes = (blocks / scale).astype(np.float32).astype(dtype).astype(np.float64)
    return np.moveaxis((codes * scale).reshape(v.shape), -1, axis)


WIDE = False


def mx_kscale(k):
    if not WIDE:
        return np.ones(k)
    levels = np.array([10, -10, 5, -5, 0])
    if k % 512:
        return np.exp2(np.random.permutation(np.resize(levels, k // 32))).repeat(32)
    a = np.empty((k // 512, 16))
    for p in range(k // 512):
        a[p, :8] = np.random.permutation(np.resize(levels, 8))
        for g in range(8):
            far = levels[np.abs(levels - a[p, g]) >= 10]
            a[p, g + 8] = far[np.random.randint(len(far))]
    return np.exp2(a.ravel()).repeat(32)


def f64(x):
    return np.asarray(x).astype(np.float64)


def striped(idx):
    return np.tile(idx.reshape(-1, 16).T, (8, 1)).astype(np.uint16)


def unstriped(offs):
    return offs[:16].T.reshape(-1).astype(np.int64)


K, T, S, N = 1024, 512, 512, 2048


def setup_inputs():
    n = np.random.standard_normal
    s = mx_kscale(K)[:, None]
    return {
        "w": (n((K, N)) / np.sqrt(K) / s).astype(np.float32),
        "xT": (n((K, T)) * s).astype(np.float32),
        "b": (0.3 * n((S, 1))).astype(np.float32),
        "offs": striped(np.sort(np.random.permutation(N)[:S])),
    }


def reference(w, xT, b, offs):
    idx = unstriped(offs)
    wq = mxq(f64(w)[:, idx], 0, "e4m3")
    return (wq.T @ mxq(f64(xT), 0, "e4m3")) + f64(b)

@@ -1,0 +1,194 @@
+from contextlib import ExitStack
+
+import concourse.mybir as mybir
+from concourse.masks import make_identity
+
+K, N, S, T = 1024, 2048, 512, 512
+FLOPS = 2 * K * S * T
+
+F32 = mybir.dt.float32
+BF16 = mybir.dt.bfloat16
+U32 = mybir.dt.uint32
+U16 = mybir.dt.uint16
+U8 = mybir.dt.uint8
+FP8X4 = mybir.dt.float8_e4m3fn_x4
+IDENTITY = mybir.ActivationFunctionType.Identity
+
+P = 128
+PACK = 4
+K_PASS = P * PACK
+PASSES = K // K_PASS
+BLOCKS = S // P
+OFFS_PER_COLUMN = 16
+
+
+def tile_picked_neuron_lin_bias_srt_e_kernel(tc, w, xT, b, offs, out):
+    nc = tc.nc
+    with ExitStack() as ctx:
+        keep = ctx.enter_context(tc.tile_pool(name="keep", bufs=1))
+        psum = ctx.enter_context(tc.psum_pool(name="psum", bufs=1))
+
+        offsets = keep.tile([P, S // OFFS_PER_COLUMN], U16, name="offsets")
+        w_raw = [keep.tile([P, PACK, N], F32, name="w_raw%d" % a) for a in range(PASSES)]
+        x_chunks = [(0, 0, 256), (1, 0, 256), (0, 256, 512), (1, 256, 512)]
+        x_raw = {(a, lo, hi): keep.tile([P, PACK, hi - lo], F32, name="x_raw%d_%d" % (a, lo)) for a, lo, hi in x_chunks}
+        w_grp = [keep.tile([P, S, PACK], BF16, name="w_grp%d" % a, align_bytes=64) for a in range(PASSES)]
+        x_grp = [keep.tile([P, T, PACK], BF16, name="x_grp%d" % a, align_bytes=64) for a in range(PASSES)]
+        g4 = keep.tile([P, PACK, S], F32, name="g4")
+        w_codes = [keep.tile([P, S], U32, name="w_codes%d" % a, align_bytes=64) for a in range(PASSES)]
+        w_scales = [keep.tile([P, S], U8, name="w_scales%d" % a, align_bytes=64) for a in range(PASSES)]
+        x_codes = [keep.tile([P, T], U32, name="x_codes%d" % a, align_bytes=64) for a in range(PASSES)]
+        x_scales = [keep.tile([P, T], U8, name="x_scales%d" % a, align_bytes=64) for a in range(PASSES)]
+        result = keep.tile([P, BLOCKS, T], F32, name="result")
+        b_rows = keep.tile([P, P], F32, name="b_rows")
+        ident = keep.tile([P, P], F32, name="ident")
+        bias = keep.tile([P, BLOCKS], F32, name="bias")
+
+        w_view = [w[a * K_PASS : (a + 1) * K_PASS, :].rearrange("(p j) n -> p j n", j=PACK) for a in range(PASSES)]
+        x_view = [xT[a * K_PASS : (a + 1) * K_PASS, :].rearrange("(p j) t -> p j t", j=PACK) for a in range(PASSES)]
+        out_view = out.rearrange("(m p) t -> p m t", p=P)
+
+        def load_w(a, j0, j1):
+            nc.sync.dma_start(out=w_raw[a][:, j0:j1, :], in_=w_view[a][:, j0:j1, :])
+
+        def load_x(a, lo, hi):
+            nc.sync.dma_start(out=x_raw[(a, lo, hi)][:], in_=x_view[a][:, :, lo:hi])
+
+        def load_offs():
+            nc.sync.dma_start(offsets[:], offs)
+
+        load_w(0, 0, 2)
+        load_offs()
+        load_w(0, 2, 4)
+        load_w(1, 0, 2)
+        load_x(0, 0, 256)
+        load_w(1, 2, 3)
+        load_w(1, 3, 4)
+        load_x(1, 0, 256)
+        load_x(0, 256, 512)
+        load_x(1, 256, 512)
+
+        nc.gpsimd.memset(b_rows[:], 0.0)
+        make_identity(nc, ident[:])
+        nc.scalar.dma_start(out=b_rows[0:BLOCKS, :], in_=b.rearrange("(m p) o -> m (p o)", p=P))
+        b_bank = psum.tile([P, 512], F32, name="bank7")
+        nc.tensor.transpose(b_bank[:, 0:P], b_rows[:], ident[:])
+        nc.scalar.copy(bias[:], b_bank[:, 0:BLOCKS])
+
+        banks = [psum.tile([P, 512], F32, name="bank%d" % i) for i in range(8)]
+
+        def gather(a, j, lo, hi):
+            nc.vector.tensor_copy(
+                w_grp[a][:, lo:hi, j],
+                w_raw[a][:, j, :].indirect(offsets[:, lo // OFFS_PER_COLUMN : hi // OFFS_PER_COLUMN]),
+            )
+
+        def gather0(j):
+            nc.vector.tensor_copy(g4[:, j, :], w_raw[0][:, j, :].indirect(offsets[:]))
+
+        def iw0(lo, hi):
+            dst, src = by_fours(w_grp[0][:, lo:hi, :], g4[:, :, lo:hi])
+            nc.scalar.copy(dst, src)
+
+        def quantize(codes, scales, grp, lo, hi):
+            nc.vector.quantize_mx(
+                out=codes[:, lo:hi].bitcast(FP8X4),
+                scales=scales[:, lo:hi],
+                in_=grp[:, lo:hi, :].rearrange("p s j -> p (s j)"),
+            )
+
+        def qw(a, lo, hi):
+            quantize(w_codes[a], w_scales[a], w_grp[a], lo, hi)
+
+        def qx(a, lo, hi):
+            quantize(x_codes[a], x_scales[a], x_grp[a], lo, hi)
+
+        def raw_part(a, lo, hi):
+            for key in x_raw:
+                if key[0] == a and key[1] <= lo and hi <= key[2]:
+                    return x_raw[key][:, :, lo - key[1] : hi - key[1]]
+            raise ValueError("no chunk")
+
+        def by_fours(grouped, raw):
+            return (
+                grouped.rearrange("p (c i) j -> p c j i", i=4),
+                raw.rearrange("p j (c i) -> p c j i", i=4),
+            )
+
+        def ixs(a, lo, hi):
+            dst, src = by_fours(x_grp[a][:, lo:hi, :], raw_part(a, lo, hi))
+            nc.scalar.copy(dst, src)
+
+        def ixv(a, lo, hi):
+            dst, src = by_fours(x_grp[a][:, lo:hi, :], raw_part(a, lo, hi))
+            nc.vector.tensor_copy(dst, src)
+
+        def bank_part(m, lo, hi):
+            if lo >= 256:
+                return banks[4 + m][:, lo - 256 : hi - 256]
+            return banks[m][:, lo:hi]
+
+        def mm(a, ms, lo, hi):
+            for m in ms:
+                cols = slice(m * P, (m + 1) * P)
+                nc.tensor.matmul_mx(
+                    out=bank_part(m, lo, hi),
+                    lhsT=w_codes[a][:, cols].bitcast(FP8X4),
+                    lhsT_scale=w_scales[a][:, cols],
+                    rhs=x_codes[a][:, lo:hi].bitcast(FP8X4),
+                    rhs_scale=x_scales[a][:, lo:hi],
+                    start=(a == 0),
+                    stop=(a == PASSES - 1),
+                )
+
+        def evs(m, lo, hi):
+            nc.scalar.activation(result[:, m, lo:hi], bank_part(m, lo, hi), IDENTITY, bias=bias[:, m : m + 1])
+
+        def evv(m, lo, hi):
+            nc.vector.tensor_scalar_add(result[:, m, lo:hi], bank_part(m, lo, hi), bias[:, m : m + 1])
+
+        def store(m0, m1, lo, hi, queue=nc.sync):
+            queue.dma_start(out=out_view[:, m0:m1, lo:hi], in_=result[:, m0:m1, lo:hi])
+
+        for j in range(PACK):
+            gather0(j)
+        iw0(0, S)
+        gather(1, 0, 0, S)
+        gather(1, 1, 0, S)
+        qw(0, 0, S)
+        ixs(0, 0, 256)
+        qx(0, 0, 256)
+        mm(0, range(4), 0, 256)
+        gather(1, 2, 0, S)
+        gather(1, 3, 0, 256)
+        gather(1, 3, 256, S)
+        qw(1, 0, 256)
+        qw(1, 256, S)
+        for m in range(BLOCKS):
+            nc.tensor.matmul_mx(
+                out=bank_part(m, 256, 512),
+                lhsT=w_codes[1][:, 0:P].bitcast(FP8X4),
+                lhsT_scale=w_scales[1][:, 0:P],
+                rhs=x_codes[0][:, 0:256].bitcast(FP8X4),
+                rhs_scale=x_scales[0][:, 0:256],
+                start=True,
+                stop=True,
+            )
+        ixs(1, 0, 256)
+        qx(1, 0, 256)
+        mm(1, range(4), 0, 256)
+        ixs(0, 256, 512)
+        for m in range(BLOCKS):
+            evs(m, 0, 256)
+        store(0, 4, 0, 256)
+        ixv(1, 256, 512)
+        qx(0, 256, 512)
+        mm(0, range(4), 256, 512)
+        qx(1, 256, 512)
+        for m in range(BLOCKS):
+            mm(1, [m], 256, 512)
+            (evs if m % 2 == 0 else evv)(m, 256, 512)
+            if m == 1:
+                store(0, 2, 256, 512)
+            if m > 1:
+                store(m, m + 1, 256, 512)

@@ -20,6 +20,8 @@ K_PASS = P * PACK
 PASSES = K // K_PASS
 BLOCKS = S // P
 OFFS_PER_COLUMN = 16
+CHUNKS = [(0, 128), (128, 256), (256, 384), (384, 512)]
+W_LOADS = [(0, 0, 2), (0, 2, 4), (1, 0, 1), (1, 1, 2), (1, 2, 3), (1, 3, 4)]
 
 
 def tile_picked_neuron_lin_bias_srt_e_kernel(tc, w, xT, b, offs, out):
@@ -28,18 +30,20 @@ def tile_picked_neuron_lin_bias_srt_e_kernel(tc, w, xT, b, offs, out):
         keep = ctx.enter_context(tc.tile_pool(name="keep", bufs=1))
         psum = ctx.enter_context(tc.psum_pool(name="psum", bufs=1))
 
+        pieces = [(a, c) for c in range(len(CHUNKS)) for a in range(PASSES)]
+        width = [hi - lo for lo, hi in CHUNKS]
         offsets = keep.tile([P, S // OFFS_PER_COLUMN], U16, name="offsets")
-        w_raw = [keep.tile([P, PACK, N], F32, name="w_raw%d" % a) for a in range(PASSES)]
-        x_chunks = [(0, 0, 256), (1, 0, 256), (0, 256, 512), (1, 256, 512)]
-        x_raw = {(a, lo, hi): keep.tile([P, PACK, hi - lo], F32, name="x_raw%d_%d" % (a, lo)) for a, lo, hi in x_chunks}
+        w_raw = {(a, j0, j1): keep.tile([P, j1 - j0, N], F32, name="w_raw%d_%d" % (a, j0)) for a, j0, j1 in W_LOADS}
+        w_slot = {(a, j): w_raw[(a, j0, j1)][:, j - j0, :] for a, j0, j1 in W_LOADS for j in range(j0, j1)}
+        x_raw = {(a, c): keep.tile([P, PACK, width[c]], F32, name="x_raw%d_%d" % (a, c), tag="x_raw%d_%d" % (a, c)) for a, c in pieces}
+        x_grp = {(a, c): keep.tile([P, width[c], PACK], BF16, name="x_grp%d_%d" % (a, c), tag="x_grp%d_%d" % (a, c), align_bytes=64) for a, c in pieces}
+        x_codes = {(a, c): keep.tile([P, width[c]], U32, name="x_codes%d_%d" % (a, c), align_bytes=64) for a, c in pieces}
+        x_scales = {(a, c): keep.tile([P, width[c]], U8, name="x_scales%d_%d" % (a, c), align_bytes=64) for a, c in pieces}
         w_grp = [keep.tile([P, S, PACK], BF16, name="w_grp%d" % a, align_bytes=64) for a in range(PASSES)]
-        x_grp = [keep.tile([P, T, PACK], BF16, name="x_grp%d" % a, align_bytes=64) for a in range(PASSES)]
         g4 = keep.tile([P, PACK, S], F32, name="g4")
-        w_codes = [keep.tile([P, S], U32, name="w_codes%d" % a, align_bytes=64) for a in range(PASSES)]
+        w_codes = {0: keep.tile([P, S], U32, name="w_codes0", align_bytes=64)}
         w_scales = [keep.tile([P, S], U8, name="w_scales%d" % a, align_bytes=64) for a in range(PASSES)]
-        x_codes = [keep.tile([P, T], U32, name="x_codes%d" % a, align_bytes=64) for a in range(PASSES)]
-        x_scales = [keep.tile([P, T], U8, name="x_scales%d" % a, align_bytes=64) for a in range(PASSES)]
-        result = keep.tile([P, BLOCKS, T], F32, name="result")
+        result = {}
         b_rows = keep.tile([P, P], F32, name="b_rows")
         ident = keep.tile([P, P], F32, name="ident")
         bias = keep.tile([P, BLOCKS], F32, name="bias")
@@ -48,66 +52,38 @@ def tile_picked_neuron_lin_bias_srt_e_kernel(tc, w, xT, b, offs, out):
         x_view = [xT[a * K_PASS : (a + 1) * K_PASS, :].rearrange("(p j) t -> p j t", j=PACK) for a in range(PASSES)]
         out_view = out.rearrange("(m p) t -> p m t", p=P)
 
-        def load_w(a, j0, j1):
-            nc.sync.dma_start(out=w_raw[a][:, j0:j1, :], in_=w_view[a][:, j0:j1, :])
+        def load_w(a, j0, j1, queue=nc.sync):
+            queue.dma_start(out=w_raw[(a, j0, j1)][:], in_=w_view[a][:, j0:j1, :])
 
-        def load_x(a, lo, hi):
-            nc.sync.dma_start(out=x_raw[(a, lo, hi)][:], in_=x_view[a][:, :, lo:hi])
+        def load_x(a, c, queue=nc.sync):
+            queue.dma_start(out=x_raw[(a, c)][:], in_=x_view[a][:, :, CHUNKS[c][0] : CHUNKS[c][1]])
 
         def load_offs():
             nc.sync.dma_start(offsets[:], offs)
 
         load_w(0, 0, 2)
         load_offs()
-        load_w(0, 2, 4)
-        load_w(1, 0, 2)
-        load_x(0, 0, 256)
-        load_w(1, 2, 3)
-        load_w(1, 3, 4)
-        load_x(1, 0, 256)
-        load_x(0, 256, 512)
-        load_x(1, 256, 512)
+        for key in W_LOADS[1:]:
+            load_w(*key)
+        for a, c in pieces:
+            load_x(a, c)
+
+        banks = [psum.tile([P, 512], F32, name="bank%d" % i) for i in range(8)]
 
         nc.gpsimd.memset(b_rows[:], 0.0)
         make_identity(nc, ident[:])
         nc.scalar.dma_start(out=b_rows[0:BLOCKS, :], in_=b.rearrange("(m p) o -> m (p o)", p=P))
-        b_bank = psum.tile([P, 512], F32, name="bank7")
-        nc.tensor.transpose(b_bank[:, 0:P], b_rows[:], ident[:])
-        nc.scalar.copy(bias[:], b_bank[:, 0:BLOCKS])
-
-        banks = [psum.tile([P, 512], F32, name="bank%d" % i) for i in range(8)]
+        nc.tensor.transpose(banks[7][:, 0:P], b_rows[:], ident[:])
+        nc.scalar.activation(bias[:], banks[7][:, 0:BLOCKS], IDENTITY)
 
         def gather(a, j, lo, hi):
             nc.vector.tensor_copy(
                 w_grp[a][:, lo:hi, j],
-                w_raw[a][:, j, :].indirect(offsets[:, lo // OFFS_PER_COLUMN : hi // OFFS_PER_COLUMN]),
+                w_slot[(a, j)].indirect(offsets[:, lo // OFFS_PER_COLUMN : hi // OFFS_PER_COLUMN]),
             )
 
         def gather0(j):
-            nc.vector.tensor_copy(g4[:, j, :], w_raw[0][:, j, :].indirect(offsets[:]))
-
-        def iw0(lo, hi):
-            dst, src = by_fours(w_grp[0][:, lo:hi, :], g4[:, :, lo:hi])
-            nc.scalar.copy(dst, src)
-
-        def quantize(codes, scales, grp, lo, hi):
-            nc.vector.quantize_mx(
-                out=codes[:, lo:hi].bitcast(FP8X4),
-                scales=scales[:, lo:hi],
-                in_=grp[:, lo:hi, :].rearrange("p s j -> p (s j)"),
-            )
-
-        def qw(a, lo, hi):
-            quantize(w_codes[a], w_scales[a], w_grp[a], lo, hi)
-
-        def qx(a, lo, hi):
-            quantize(x_codes[a], x_scales[a], x_grp[a], lo, hi)
-
-        def raw_part(a, lo, hi):
-            for key in x_raw:
-                if key[0] == a and key[1] <= lo and hi <= key[2]:
-                    return x_raw[key][:, :, lo - key[1] : hi - key[1]]
-            raise ValueError("no chunk")
+            nc.vector.tensor_copy(g4[:, j, :], w_slot[(0, j)].indirect(offsets[:]))
 
         def by_fours(grouped, raw):
             return (
@@ -115,40 +91,60 @@ def tile_picked_neuron_lin_bias_srt_e_kernel(tc, w, xT, b, offs, out):
                 raw.rearrange("p j (c i) -> p c j i", i=4),
             )
 
-        def ixs(a, lo, hi):
-            dst, src = by_fours(x_grp[a][:, lo:hi, :], raw_part(a, lo, hi))
+        def iw0(lo, hi):
+            dst, src = by_fours(w_grp[0][:, lo:hi, :], g4[:, :, lo:hi])
             nc.scalar.copy(dst, src)
 
-        def ixv(a, lo, hi):
-            dst, src = by_fours(x_grp[a][:, lo:hi, :], raw_part(a, lo, hi))
+        def quantize(codes, scales, grp):
+            nc.vector.quantize_mx(out=codes.bitcast(FP8X4), scales=scales, in_=grp.rearrange("p s j -> p (s j)"))
+
+        def open_w_codes(after):
+            w_codes[1] = keep.tile([P, S], U32, name="w_codes1", tag="x_grp%d_%d" % after, align_bytes=64)
+
+        def qw(a, lo, hi):
+            quantize(w_codes[a][:, lo:hi], w_scales[a][:, lo:hi], w_grp[a][:, lo:hi, :])
+
+        def qx(a, c):
+            quantize(x_codes[(a, c)][:], x_scales[(a, c)][:], x_grp[(a, c)][:])
+
+        def ixs(a, c, lo=0, hi=None):
+            hi = width[c] if hi is None else hi
+            dst, src = by_fours(x_grp[(a, c)][:, lo:hi, :], x_raw[(a, c)][:, :, lo:hi])
+            nc.scalar.copy(dst, src)
+
+        def ixv(a, c, lo=0, hi=None):
+            hi = width[c] if hi is None else hi
+            dst, src = by_fours(x_grp[(a, c)][:, lo:hi, :], x_raw[(a, c)][:, :, lo:hi])
             nc.vector.tensor_copy(dst, src)
 
-        def bank_part(m, lo, hi):
-            if lo >= 256:
-                return banks[4 + m][:, lo - 256 : hi - 256]
-            return banks[m][:, lo:hi]
+        def acc(c, m):
+            return banks[4 * (c % 2) + m][:, (c // 2) * P : (c // 2 + 1) * P]
 
-        def mm(a, ms, lo, hi):
+        def mm(a, c, ms, first=0):
             for m in ms:
                 cols = slice(m * P, (m + 1) * P)
                 nc.tensor.matmul_mx(
-                    out=bank_part(m, lo, hi),
+                    out=acc(c, m),
                     lhsT=w_codes[a][:, cols].bitcast(FP8X4),
                     lhsT_scale=w_scales[a][:, cols],
-                    rhs=x_codes[a][:, lo:hi].bitcast(FP8X4),
-                    rhs_scale=x_scales[a][:, lo:hi],
-                    start=(a == 0),
-                    stop=(a == PASSES - 1),
+                    rhs=x_codes[(a, c)][:].bitcast(FP8X4),
+                    rhs_scale=x_scales[(a, c)][:],
+                    start=(a == first),
+                    stop=(a != first),
                 )
 
-        def evs(m, lo, hi):
-            nc.scalar.activation(result[:, m, lo:hi], bank_part(m, lo, hi), IDENTITY, bias=bias[:, m : m + 1])
+        def open_result(c, after=None):
+            tag = "result%d" % c if after is None else "x_raw%d_%d" % after
+            result[c] = keep.tile([P, BLOCKS, width[c]], F32, name="result%d" % c, tag=tag)
 
-        def evv(m, lo, hi):
-            nc.vector.tensor_scalar_add(result[:, m, lo:hi], bank_part(m, lo, hi), bias[:, m : m + 1])
+        def evs(c, m):
+            nc.scalar.activation(result[c][:, m, :], acc(c, m), IDENTITY, bias=bias[:, m : m + 1])
 
-        def store(m0, m1, lo, hi, queue=nc.sync):
-            queue.dma_start(out=out_view[:, m0:m1, lo:hi], in_=result[:, m0:m1, lo:hi])
+        def evv(c, m):
+            nc.vector.tensor_scalar_add(result[c][:, m, :], acc(c, m), bias[:, m : m + 1])
+
+        def store(c, m0, m1, queue=nc.sync):
+            queue.dma_start(out=out_view[:, m0:m1, CHUNKS[c][0] : CHUNKS[c][1]], in_=result[c][:, m0:m1, :])
 
         for j in range(PACK):
             gather0(j)
@@ -156,39 +152,49 @@ def tile_picked_neuron_lin_bias_srt_e_kernel(tc, w, xT, b, offs, out):
         gather(1, 0, 0, S)
         gather(1, 1, 0, S)
         qw(0, 0, S)
-        ixs(0, 0, 256)
-        qx(0, 0, 256)
-        mm(0, range(4), 0, 256)
         gather(1, 2, 0, S)
         gather(1, 3, 0, 256)
+        ixs(0, 0)
+        ixs(1, 0)
         gather(1, 3, 256, S)
+        qx(0, 0)
+        mm(0, 0, range(4))
+        open_w_codes((0, 0))
         qw(1, 0, 256)
+        qx(1, 0)
         qw(1, 256, S)
+        mm(1, 0, range(4))
+        ixs(0, 1)
+        ixs(1, 1)
+        qx(0, 1)
+        mm(0, 1, range(4))
+        ixv(0, 2)
+        qx(1, 1)
+        mm(1, 1, range(4))
+        open_result(0, (1, 1))
         for m in range(BLOCKS):
-            nc.tensor.matmul_mx(
-                out=bank_part(m, 256, 512),
-                lhsT=w_codes[1][:, 0:P].bitcast(FP8X4),
-                lhsT_scale=w_scales[1][:, 0:P],
-                rhs=x_codes[0][:, 0:256].bitcast(FP8X4),
-                rhs_scale=x_scales[0][:, 0:256],
-                start=True,
-                stop=True,
-            )
-        ixs(1, 0, 256)
-        qx(1, 0, 256)
-        mm(1, range(4), 0, 256)
-        ixs(0, 256, 512)
+            evs(0, m)
+        store(0, 0, 4)
+        ixv(1, 2)
+        qx(0, 2)
+        mm(0, 2, range(4))
+        qx(1, 2)
+        mm(1, 2, range(4))
+        ixv(0, 3)
+        open_result(1)
         for m in range(BLOCKS):
-            evs(m, 0, 256)
-        store(0, 4, 0, 256)
-        ixv(1, 256, 512)
-        qx(0, 256, 512)
-        mm(0, range(4), 256, 512)
-        qx(1, 256, 512)
+            evs(1, m)
+        store(1, 0, 4)
+        ixv(1, 3)
+        qx(0, 3)
+        mm(0, 3, range(4))
+        qx(1, 3)
+        mm(1, 3, range(4))
+        open_result(2)
         for m in range(BLOCKS):
-            mm(1, [m], 256, 512)
-            (evs if m % 2 == 0 else evv)(m, 256, 512)
-            if m == 1:
-                store(0, 2, 256, 512)
-            if m > 1:
-                store(m, m + 1, 256, 512)
+            evs(2, m)
+        store(2, 0, 4)
+        open_result(3)
+        for m in range(BLOCKS):
+            (evs if m % 2 == 1 else evv)(3, m)
+        store(3, 0, 4)

@@ -1,7 +1,6 @@
 from contextlib import ExitStack
 
 import concourse.mybir as mybir
-from concourse.masks import make_identity
 
 K, N, S, T = 1024, 2048, 512, 512
 FLOPS = 2 * K * S * T
@@ -44,9 +43,8 @@ def tile_picked_neuron_lin_bias_srt_e_kernel(tc, w, xT, b, offs, out):
         w_codes = {0: keep.tile([P, S], U32, name="w_codes0", align_bytes=64)}
         w_scales = [keep.tile([P, S], U8, name="w_scales%d" % a, align_bytes=64) for a in range(PASSES)]
         result = {}
-        b_rows = keep.tile([P, P], F32, name="b_rows")
-        ident = keep.tile([P, P], F32, name="ident")
-        bias = keep.tile([P, BLOCKS], F32, name="bias")
+        b_rows = keep.tile([P, BLOCKS * 32], F32, name="b_rows", align_bytes=64)
+        b_cols = keep.tile([P, BLOCKS * 32], F32, name="b_cols", align_bytes=64)
 
         w_view = [w[a * K_PASS : (a + 1) * K_PASS, :].rearrange("(p j) n -> p j n", j=PACK) for a in range(PASSES)]
         x_view = [xT[a * K_PASS : (a + 1) * K_PASS, :].rearrange("(p j) t -> p j t", j=PACK) for a in range(PASSES)]
@@ -58,23 +56,26 @@ def tile_picked_neuron_lin_bias_srt_e_kernel(tc, w, xT, b, offs, out):
         def load_x(a, c, queue=nc.sync):
             queue.dma_start(out=x_raw[(a, c)][:], in_=x_view[a][:, :, CHUNKS[c][0] : CHUNKS[c][1]])
 
+        def load_bias():
+            nc.vector.memset(b_rows[:], 0.0)
+            nc.sync.dma_start(
+                out=b_rows[0:P:32, :].rearrange("q (m c) -> q m c", c=32),
+                in_=b.rearrange("(m q c) o -> q m (c o)", m=BLOCKS, c=32),
+            )
+            nc.vector.transpose(b_cols[:], b_rows[:])
+
         def load_offs():
             nc.sync.dma_start(offsets[:], offs)
 
         load_w(0, 0, 2)
         load_offs()
+        load_bias()
         for key in W_LOADS[1:]:
             load_w(*key)
         for a, c in pieces:
             load_x(a, c)
 
         banks = [psum.tile([P, 512], F32, name="bank%d" % i) for i in range(8)]
-
-        nc.gpsimd.memset(b_rows[:], 0.0)
-        make_identity(nc, ident[:])
-        nc.scalar.dma_start(out=b_rows[0:BLOCKS, :], in_=b.rearrange("(m p) o -> m (p o)", p=P))
-        nc.tensor.transpose(banks[7][:, 0:P], b_rows[:], ident[:])
-        nc.scalar.activation(bias[:], banks[7][:, 0:BLOCKS], IDENTITY)
 
         def gather(a, j, lo, hi):
             nc.vector.tensor_copy(
@@ -138,10 +139,10 @@ def tile_picked_neuron_lin_bias_srt_e_kernel(tc, w, xT, b, offs, out):
             result[c] = keep.tile([P, BLOCKS, width[c]], F32, name="result%d" % c, tag=tag)
 
         def evs(c, m):
-            nc.scalar.activation(result[c][:, m, :], acc(c, m), IDENTITY, bias=bias[:, m : m + 1])
+            nc.scalar.activation(result[c][:, m, :], acc(c, m), IDENTITY, bias=b_cols[:, 32 * m : 32 * m + 1])
 
         def evv(c, m):
-            nc.vector.tensor_scalar_add(result[c][:, m, :], acc(c, m), bias[:, m : m + 1])
+            nc.vector.tensor_scalar_add(result[c][:, m, :], acc(c, m), b_cols[:, 32 * m : 32 * m + 1])
 
         def store(c, m0, m1, queue=nc.sync):
             queue.dma_start(out=out_view[:, m0:m1, CHUNKS[c][0] : CHUNKS[c][1]], in_=result[c][:, m0:m1, :])
@@ -197,4 +198,5 @@ def tile_picked_neuron_lin_bias_srt_e_kernel(tc, w, xT, b, offs, out):
         open_result(3)
         for m in range(BLOCKS):
             (evs if m % 2 == 1 else evv)(3, m)
-        store(3, 0, 4)
+            if m % 2 == 1:
+                store(3, m - 1, m + 1)

@@ -19,7 +19,7 @@ K_PASS = P * PACK
 PASSES = K // K_PASS
 BLOCKS = S // P
 OFFS_PER_COLUMN = 16
-CHUNKS = [(0, 128), (128, 256), (256, 384), (384, 512)]
+CHUNKS = [(0, 128), (128, 256), (256, 384), (384, 448), (448, 512)]
 W_LOADS = [(0, 0, 2), (0, 2, 4), (1, 0, 1), (1, 1, 2), (1, 2, 3), (1, 3, 4)]
 
 
@@ -32,15 +32,16 @@ def tile_picked_neuron_lin_bias_srt_e_kernel(tc, w, xT, b, offs, out):
         pieces = [(a, c) for c in range(len(CHUNKS)) for a in range(PASSES)]
         width = [hi - lo for lo, hi in CHUNKS]
         offsets = keep.tile([P, S // OFFS_PER_COLUMN], U16, name="offsets")
-        w_raw = {(a, j0, j1): keep.tile([P, j1 - j0, N], F32, name="w_raw%d_%d" % (a, j0)) for a, j0, j1 in W_LOADS}
+        w_raw = {(a, j0, j1): keep.tile([P, j1 - j0, N], F32, name="w_raw%d_%d" % (a, j0), tag="w_raw%d_%d" % (a, j0), align_bytes=64) for a, j0, j1 in W_LOADS}
         w_slot = {(a, j): w_raw[(a, j0, j1)][:, j - j0, :] for a, j0, j1 in W_LOADS for j in range(j0, j1)}
-        x_raw = {(a, c): keep.tile([P, PACK, width[c]], F32, name="x_raw%d_%d" % (a, c), tag="x_raw%d_%d" % (a, c)) for a, c in pieces}
+        x_raw = {(a, c): keep.tile([P, PACK, width[c]], F32, name="x_raw%d_%d" % (a, c), tag="x_raw%d_%d" % (a, c), align_bytes=64) for a, c in pieces}
         x_grp = {(a, c): keep.tile([P, width[c], PACK], BF16, name="x_grp%d_%d" % (a, c), tag="x_grp%d_%d" % (a, c), align_bytes=64) for a, c in pieces}
-        x_codes = {(a, c): keep.tile([P, width[c]], U32, name="x_codes%d_%d" % (a, c), align_bytes=64) for a, c in pieces}
-        x_scales = {(a, c): keep.tile([P, width[c]], U8, name="x_scales%d_%d" % (a, c), align_bytes=64) for a, c in pieces}
+        x_codes = [keep.tile([P, T], U32, name="x_codes%d" % a, align_bytes=64) for a in range(PASSES)]
+        x_scales = [keep.tile([P, T], U8, name="x_scales%d" % a, align_bytes=64) for a in range(PASSES)]
         w_grp = [keep.tile([P, S, PACK], BF16, name="w_grp%d" % a, align_bytes=64) for a in range(PASSES)]
         g4 = keep.tile([P, PACK, S], F32, name="g4")
-        w_codes = {0: keep.tile([P, S], U32, name="w_codes0", align_bytes=64)}
+        HALF = S // 2
+        w_codes = {}
         w_scales = [keep.tile([P, S], U8, name="w_scales%d" % a, align_bytes=64) for a in range(PASSES)]
         result = {}
         b_rows = keep.tile([P, BLOCKS * 32], F32, name="b_rows", align_bytes=64)
@@ -99,14 +100,18 @@ def tile_picked_neuron_lin_bias_srt_e_kernel(tc, w, xT, b, offs, out):
         def quantize(codes, scales, grp):
             nc.vector.quantize_mx(out=codes.bitcast(FP8X4), scales=scales, in_=grp.rearrange("p s j -> p (s j)"))
 
-        def open_w_codes(after):
-            w_codes[1] = keep.tile([P, S], U32, name="w_codes1", tag="x_grp%d_%d" % after, align_bytes=64)
+        def open_w_codes(a, lo, hi, tag):
+            t = keep.tile([P, hi - lo], U32, name="w_codes%d_%d" % (a, lo), tag=tag, align_bytes=64)
+            for m in range(lo // P, hi // P):
+                w_codes[(a, m)] = t[:, m * P - lo : (m + 1) * P - lo]
+            w_codes[(a, lo, hi)] = t
 
         def qw(a, lo, hi):
-            quantize(w_codes[a][:, lo:hi], w_scales[a][:, lo:hi], w_grp[a][:, lo:hi, :])
+            quantize(w_codes[(a, lo, hi)][:], w_scales[a][:, lo:hi], w_grp[a][:, lo:hi, :])
 
         def qx(a, c):
-            quantize(x_codes[(a, c)][:], x_scales[(a, c)][:], x_grp[(a, c)][:])
+            lo, hi = CHUNKS[c]
+            quantize(x_codes[a][:, lo:hi], x_scales[a][:, lo:hi], x_grp[(a, c)][:])
 
         def ixs(a, c, lo=0, hi=None):
             hi = width[c] if hi is None else hi
@@ -121,28 +126,31 @@ def tile_picked_neuron_lin_bias_srt_e_kernel(tc, w, xT, b, offs, out):
         def acc(c, m):
             return banks[4 * (c % 2) + m][:, (c // 2) * P : (c // 2 + 1) * P]
 
+        def acc_real(c, m):
+            return acc(c, m)[:, P - width[c] : P]
+
         def mm(a, c, ms, first=0):
             for m in ms:
                 cols = slice(m * P, (m + 1) * P)
                 nc.tensor.matmul_mx(
                     out=acc(c, m),
-                    lhsT=w_codes[a][:, cols].bitcast(FP8X4),
+                    lhsT=w_codes[(a, m)].bitcast(FP8X4),
                     lhsT_scale=w_scales[a][:, cols],
-                    rhs=x_codes[(a, c)][:].bitcast(FP8X4),
-                    rhs_scale=x_scales[(a, c)][:],
+                    rhs=x_codes[a][:, CHUNKS[c][1] - P : CHUNKS[c][1]].bitcast(FP8X4),
+                    rhs_scale=x_scales[a][:, CHUNKS[c][1] - P : CHUNKS[c][1]],
                     start=(a == first),
                     stop=(a != first),
                 )
 
         def open_result(c, after=None):
             tag = "result%d" % c if after is None else "x_raw%d_%d" % after
-            result[c] = keep.tile([P, BLOCKS, width[c]], F32, name="result%d" % c, tag=tag)
+            result[c] = keep.tile([P, BLOCKS, width[c]], F32, name="result%d" % c, tag=tag, align_bytes=64)
 
         def evs(c, m):
-            nc.scalar.activation(result[c][:, m, :], acc(c, m), IDENTITY, bias=b_cols[:, 32 * m : 32 * m + 1])
+            nc.scalar.activation(result[c][:, m, :], acc_real(c, m), IDENTITY, bias=b_cols[:, 32 * m : 32 * m + 1])
 
         def evv(c, m):
-            nc.vector.tensor_scalar_add(result[c][:, m, :], acc(c, m), b_cols[:, 32 * m : 32 * m + 1])
+            nc.vector.tensor_scalar_add(result[c][:, m, :], acc_real(c, m), b_cols[:, 32 * m : 32 * m + 1])
 
         def store(c, m0, m1, queue=nc.sync):
             queue.dma_start(out=out_view[:, m0:m1, CHUNKS[c][0] : CHUNKS[c][1]], in_=result[c][:, m0:m1, :])
@@ -152,18 +160,20 @@ def tile_picked_neuron_lin_bias_srt_e_kernel(tc, w, xT, b, offs, out):
         iw0(0, S)
         gather(1, 0, 0, S)
         gather(1, 1, 0, S)
+        open_w_codes(0, 0, S, "w_codes0")
         qw(0, 0, S)
         gather(1, 2, 0, S)
-        gather(1, 3, 0, 256)
+        gather(1, 3, 0, HALF)
         ixs(0, 0)
         ixs(1, 0)
-        gather(1, 3, 256, S)
+        gather(1, 3, HALF, S)
         qx(0, 0)
         mm(0, 0, range(4))
-        open_w_codes((0, 0))
-        qw(1, 0, 256)
+        open_w_codes(1, 0, HALF, "x_grp0_0")
+        qw(1, 0, HALF)
         qx(1, 0)
-        qw(1, 256, S)
+        open_w_codes(1, HALF, S, "x_grp1_0")
+        qw(1, HALF, S)
         mm(1, 0, range(4))
         ixs(0, 1)
         ixs(1, 1)
@@ -179,9 +189,9 @@ def tile_picked_neuron_lin_bias_srt_e_kernel(tc, w, xT, b, offs, out):
         ixv(1, 2)
         qx(0, 2)
         mm(0, 2, range(4))
+        ixv(0, 3)
         qx(1, 2)
         mm(1, 2, range(4))
-        ixv(0, 3)
         open_result(1)
         for m in range(BLOCKS):
             evs(1, m)
@@ -189,14 +199,24 @@ def tile_picked_neuron_lin_bias_srt_e_kernel(tc, w, xT, b, offs, out):
         ixv(1, 3)
         qx(0, 3)
         mm(0, 3, range(4))
+        ixv(0, 4)
         qx(1, 3)
         mm(1, 3, range(4))
         open_result(2)
         for m in range(BLOCKS):
             evs(2, m)
-        store(2, 0, 4)
+            if m % 2 == 1:
+                store(2, m - 1, m + 1)
+        ixv(1, 4)
+        qx(0, 4)
+        mm(0, 4, range(4))
+        qx(1, 4)
+        mm(1, 4, range(4))
         open_result(3)
         for m in range(BLOCKS):
-            (evs if m % 2 == 1 else evv)(3, m)
-            if m % 2 == 1:
-                store(3, m - 1, m + 1)
+            evs(3, m)
+        store(3, 0, 4)
+        open_result(4)
+        for m in range(BLOCKS):
+            (evs if m % 2 == 1 else evv)(4, m)
+        store(4, 0, 4)

@@ -20,7 +20,6 @@ PASSES = K // K_PASS
 BLOCKS = S // P
 OFFS_PER_COLUMN = 16
 CHUNKS = [(0, 128), (128, 256), (256, 384), (384, 448), (448, 512)]
-W_LOADS = [(0, 0, 2), (0, 2, 4), (1, 0, 1), (1, 1, 2), (1, 2, 3), (1, 3, 4)]
 
 
 def tile_picked_neuron_lin_bias_srt_e_kernel(tc, w, xT, b, offs, out):
@@ -32,8 +31,14 @@ def tile_picked_neuron_lin_bias_srt_e_kernel(tc, w, xT, b, offs, out):
         pieces = [(a, c) for c in range(len(CHUNKS)) for a in range(PASSES)]
         width = [hi - lo for lo, hi in CHUNKS]
         offsets = keep.tile([P, S // OFFS_PER_COLUMN], U16, name="offsets")
-        w_raw = {(a, j0, j1): keep.tile([P, j1 - j0, N], F32, name="w_raw%d_%d" % (a, j0), tag="w_raw%d_%d" % (a, j0), align_bytes=64) for a, j0, j1 in W_LOADS}
-        w_slot = {(a, j): w_raw[(a, j0, j1)][:, j - j0, :] for a, j0, j1 in W_LOADS for j in range(j0, j1)}
+        w_first = keep.tile([P, PACK - 1, N], F32, name="w_first")
+        w_last_slots = keep.tile([P, PASSES, N], F32, name="w_last_slots")
+        w_single = [keep.tile([P, N], F32, name="w_single%d" % j) for j in range(PACK - 1)]
+        w_slot = {
+            (a, j): w_last_slots[:, a, :] if j == PACK - 1 else (w_first[:, j, :] if a == 0 else w_single[j][:])
+            for a in range(PASSES)
+            for j in range(PACK)
+        }
         x_raw = {(a, c): keep.tile([P, PACK, width[c]], F32, name="x_raw%d_%d" % (a, c), tag="x_raw%d_%d" % (a, c), align_bytes=64) for a, c in pieces}
         x_grp = {(a, c): keep.tile([P, width[c], PACK], BF16, name="x_grp%d_%d" % (a, c), tag="x_grp%d_%d" % (a, c), align_bytes=64) for a, c in pieces}
         x_codes = [keep.tile([P, T], U32, name="x_codes%d" % a, align_bytes=64) for a in range(PASSES)]
@@ -51,9 +56,6 @@ def tile_picked_neuron_lin_bias_srt_e_kernel(tc, w, xT, b, offs, out):
         x_view = [xT[a * K_PASS : (a + 1) * K_PASS, :].rearrange("(p j) t -> p j t", j=PACK) for a in range(PASSES)]
         out_view = out.rearrange("(m p) t -> p m t", p=P)
 
-        def load_w(a, j0, j1, queue=nc.sync):
-            queue.dma_start(out=w_raw[(a, j0, j1)][:], in_=w_view[a][:, j0:j1, :])
-
         def load_x(a, c, queue=nc.sync):
             queue.dma_start(out=x_raw[(a, c)][:], in_=x_view[a][:, :, CHUNKS[c][0] : CHUNKS[c][1]])
 
@@ -68,11 +70,12 @@ def tile_picked_neuron_lin_bias_srt_e_kernel(tc, w, xT, b, offs, out):
         def load_offs():
             nc.sync.dma_start(offsets[:], offs)
 
-        load_w(0, 0, 2)
+        nc.sync.dma_start(out=w_first[:], in_=w_view[0][:, 0 : PACK - 1, :])
         load_offs()
         load_bias()
-        for key in W_LOADS[1:]:
-            load_w(*key)
+        nc.sync.dma_start(out=w_last_slots[:], in_=w.rearrange("(a p j) n -> p a j n", p=P, j=PACK)[:, :, PACK - 1, :])
+        for j in range(PACK - 1):
+            nc.sync.dma_start(out=w_single[j][:], in_=w_view[1][:, j, :])
         for a, c in pieces:
             load_x(a, c)
 
@@ -158,15 +161,15 @@ def tile_picked_neuron_lin_bias_srt_e_kernel(tc, w, xT, b, offs, out):
         for j in range(PACK):
             gather0(j)
         iw0(0, S)
+        gather(1, 3, 0, S)
         gather(1, 0, 0, S)
-        gather(1, 1, 0, S)
         open_w_codes(0, 0, S, "w_codes0")
         qw(0, 0, S)
-        gather(1, 2, 0, S)
-        gather(1, 3, 0, HALF)
+        gather(1, 1, 0, S)
+        gather(1, 2, 0, HALF)
         ixs(0, 0)
         ixs(1, 0)
-        gather(1, 3, HALF, S)
+        gather(1, 2, HALF, S)
         qx(0, 0)
         mm(0, 0, range(4))
         open_w_codes(1, 0, HALF, "x_grp0_0")

@@ -28,7 +28,7 @@ def tile_picked_neuron_lin_bias_srt_e_kernel(tc, w, xT, b, offs, out):
         keep = ctx.enter_context(tc.tile_pool(name="keep", bufs=1))
         psum = ctx.enter_context(tc.psum_pool(name="psum", bufs=1))
 
-        pieces = [(a, c) for c in range(len(CHUNKS)) for a in range(PASSES)]
+        pieces = [(0, 0), (0, 1), (1, 0), (1, 1)] + [(a, c) for c in range(2, len(CHUNKS)) for a in range(PASSES)]
         width = [hi - lo for lo, hi in CHUNKS]
         offsets = keep.tile([P, S // OFFS_PER_COLUMN], U16, name="offsets")
         w_first = keep.tile([P, PACK - 1, N], F32, name="w_first")
@@ -168,20 +168,20 @@ def tile_picked_neuron_lin_bias_srt_e_kernel(tc, w, xT, b, offs, out):
         gather(1, 1, 0, S)
         gather(1, 2, 0, HALF)
         ixs(0, 0)
-        ixs(1, 0)
+        ixs(0, 1)
         gather(1, 2, HALF, S)
         qx(0, 0)
         mm(0, 0, range(4))
         open_w_codes(1, 0, HALF, "x_grp0_0")
         qw(1, 0, HALF)
-        qx(1, 0)
-        open_w_codes(1, HALF, S, "x_grp1_0")
-        qw(1, HALF, S)
-        mm(1, 0, range(4))
-        ixs(0, 1)
-        ixs(1, 1)
         qx(0, 1)
         mm(0, 1, range(4))
+        open_w_codes(1, HALF, S, "x_grp0_1")
+        qw(1, HALF, S)
+        ixs(1, 0)
+        ixs(1, 1)
+        qx(1, 0)
+        mm(1, 0, range(4))
         ixv(0, 2)
         qx(1, 1)
         mm(1, 1, range(4))

@@ -19,6 +19,7 @@ K_PASS = P * PACK
 PASSES = K // K_PASS
 BLOCKS = S // P
 OFFS_PER_COLUMN = 16
+ALIGN = 256
 CHUNKS = [(0, 128), (128, 256), (256, 384), (384, 448), (448, 512)]
 
 
@@ -30,27 +31,27 @@ def tile_picked_neuron_lin_bias_srt_e_kernel(tc, w, xT, b, offs, out):
 
         pieces = [(0, 0), (0, 1), (1, 0), (1, 1)] + [(a, c) for c in range(2, len(CHUNKS)) for a in range(PASSES)]
         width = [hi - lo for lo, hi in CHUNKS]
-        offsets = keep.tile([P, S // OFFS_PER_COLUMN], U16, name="offsets")
-        w_first = keep.tile([P, PACK - 1, N], F32, name="w_first")
-        w_last_slots = keep.tile([P, PASSES, N], F32, name="w_last_slots")
-        w_single = [keep.tile([P, N], F32, name="w_single%d" % j) for j in range(PACK - 1)]
+        offsets = keep.tile([P, S // OFFS_PER_COLUMN], U16, name="offsets", align_bytes=ALIGN)
+        w_first = keep.tile([P, PACK - 1, N], F32, name="w_first", align_bytes=ALIGN)
+        w_last_slots = keep.tile([P, PASSES, N], F32, name="w_last_slots", align_bytes=ALIGN)
+        w_single = [keep.tile([P, N], F32, name="w_single%d" % j, align_bytes=ALIGN) for j in range(PACK - 1)]
         w_slot = {
             (a, j): w_last_slots[:, a, :] if j == PACK - 1 else (w_first[:, j, :] if a == 0 else w_single[j][:])
             for a in range(PASSES)
             for j in range(PACK)
         }
-        x_raw = {(a, c): keep.tile([P, PACK, width[c]], F32, name="x_raw%d_%d" % (a, c), tag="x_raw%d_%d" % (a, c), align_bytes=64) for a, c in pieces}
-        x_grp = {(a, c): keep.tile([P, width[c], PACK], BF16, name="x_grp%d_%d" % (a, c), tag="x_grp%d_%d" % (a, c), align_bytes=64) for a, c in pieces}
-        x_codes = [keep.tile([P, T], U32, name="x_codes%d" % a, align_bytes=64) for a in range(PASSES)]
-        x_scales = [keep.tile([P, T], U8, name="x_scales%d" % a, align_bytes=64) for a in range(PASSES)]
-        w_grp = [keep.tile([P, S, PACK], BF16, name="w_grp%d" % a, align_bytes=64) for a in range(PASSES)]
-        g4 = keep.tile([P, PACK, S], F32, name="g4")
+        x_raw = {(a, c): keep.tile([P, PACK, width[c]], F32, name="x_raw%d_%d" % (a, c), tag="x_raw%d_%d" % (a, c), align_bytes=ALIGN) for a, c in pieces}
+        x_grp = {(a, c): keep.tile([P, width[c], PACK], BF16, name="x_grp%d_%d" % (a, c), tag="x_grp%d_%d" % (a, c), align_bytes=ALIGN) for a, c in pieces}
+        x_codes = [keep.tile([P, T], U32, name="x_codes%d" % a, align_bytes=ALIGN) for a in range(PASSES)]
+        x_scales = [keep.tile([P, T], U8, name="x_scales%d" % a, align_bytes=ALIGN) for a in range(PASSES)]
+        w_grp = [keep.tile([P, S, PACK], BF16, name="w_grp%d" % a, align_bytes=ALIGN) for a in range(PASSES)]
+        g4 = keep.tile([P, PACK, S], F32, name="g4", align_bytes=ALIGN)
         HALF = S // 2
         w_codes = {}
-        w_scales = [keep.tile([P, S], U8, name="w_scales%d" % a, align_bytes=64) for a in range(PASSES)]
+        w_scales = [keep.tile([P, S], U8, name="w_scales%d" % a, align_bytes=ALIGN) for a in range(PASSES)]
         result = {}
-        b_rows = keep.tile([P, BLOCKS * 32], F32, name="b_rows", align_bytes=64)
-        b_cols = keep.tile([P, BLOCKS * 32], F32, name="b_cols", align_bytes=64)
+        b_rows = keep.tile([P, BLOCKS * 32], F32, name="b_rows", align_bytes=ALIGN)
+        b_cols = keep.tile([P, BLOCKS * 32], F32, name="b_cols", align_bytes=ALIGN)
 
         w_view = [w[a * K_PASS : (a + 1) * K_PASS, :].rearrange("(p j) n -> p j n", j=PACK) for a in range(PASSES)]
         x_view = [xT[a * K_PASS : (a + 1) * K_PASS, :].rearrange("(p j) t -> p j t", j=PACK) for a in range(PASSES)]
@@ -104,7 +105,7 @@ def tile_picked_neuron_lin_bias_srt_e_kernel(tc, w, xT, b, offs, out):
             nc.vector.quantize_mx(out=codes.bitcast(FP8X4), scales=scales, in_=grp.rearrange("p s j -> p (s j)"))
 
         def open_w_codes(a, lo, hi, tag):
-            t = keep.tile([P, hi - lo], U32, name="w_codes%d_%d" % (a, lo), tag=tag, align_bytes=64)
+            t = keep.tile([P, hi - lo], U32, name="w_codes%d_%d" % (a, lo), tag=tag, align_bytes=ALIGN)
             for m in range(lo // P, hi // P):
                 w_codes[(a, m)] = t[:, m * P - lo : (m + 1) * P - lo]
             w_codes[(a, lo, hi)] = t
@@ -147,7 +148,7 @@ def tile_picked_neuron_lin_bias_srt_e_kernel(tc, w, xT, b, offs, out):
 
         def open_result(c, after=None):
             tag = "result%d" % c if after is None else "x_raw%d_%d" % after
-            result[c] = keep.tile([P, BLOCKS, width[c]], F32, name="result%d" % c, tag=tag, align_bytes=64)
+            result[c] = keep.tile([P, BLOCKS, width[c]], F32, name="result%d" % c, tag=tag, align_bytes=ALIGN)
 
         def evs(c, m):
             nc.scalar.activation(result[c][:, m, :], acc_real(c, m), IDENTITY, bias=b_cols[:, 32 * m : 32 * m + 1])

@@ -12,6 +12,7 @@ U16 = mybir.dt.uint16
 U8 = mybir.dt.uint8
 FP8X4 = mybir.dt.float8_e4m3fn_x4
 IDENTITY = mybir.ActivationFunctionType.Identity
+COPY = mybir.ActivationFunctionType.Copy
 
 P = 128
 PACK = 4
@@ -29,7 +30,7 @@ def tile_picked_neuron_lin_bias_srt_e_kernel(tc, w, xT, b, offs, out):
         keep = ctx.enter_context(tc.tile_pool(name="keep", bufs=1))
         psum = ctx.enter_context(tc.psum_pool(name="psum", bufs=1))
 
-        pieces = [(0, 0), (0, 1), (1, 0), (1, 1)] + [(a, c) for c in range(2, len(CHUNKS)) for a in range(PASSES)]
+        pieces = [(a, c) for c in range(len(CHUNKS)) for a in range(PASSES)]
         width = [hi - lo for lo, hi in CHUNKS]
         offsets = keep.tile([P, S // OFFS_PER_COLUMN], U16, name="offsets", align_bytes=ALIGN)
         w_first = keep.tile([P, PACK - 1, N], F32, name="w_first", align_bytes=ALIGN)
@@ -61,7 +62,9 @@ def tile_picked_neuron_lin_bias_srt_e_kernel(tc, w, xT, b, offs, out):
             queue.dma_start(out=x_raw[(a, c)][:], in_=x_view[a][:, :, CHUNKS[c][0] : CHUNKS[c][1]])
 
         def load_bias():
-            nc.vector.memset(b_rows[:], 0.0)
+            zero = keep.tile([P, 1], F32, name="zero", align_bytes=ALIGN)
+            nc.vector.memset(zero[:], 0.0)
+            nc.scalar.activation(b_rows[:], zero[:].to_broadcast([P, BLOCKS * 32]), COPY)
             nc.sync.dma_start(
                 out=b_rows[0:P:32, :].rearrange("q (m c) -> q m c", c=32),
                 in_=b.rearrange("(m q c) o -> q m (c o)", m=BLOCKS, c=32),
@@ -159,8 +162,9 @@ def tile_picked_neuron_lin_bias_srt_e_kernel(tc, w, xT, b, offs, out):
         def store(c, m0, m1, queue=nc.sync):
             queue.dma_start(out=out_view[:, m0:m1, CHUNKS[c][0] : CHUNKS[c][1]], in_=result[c][:, m0:m1, :])
 
-        for j in range(PACK):
+        for j in range(PACK - 1):
             gather0(j)
+        nc.scalar.activation(g4[:, PACK - 1, :], w_slot[(0, PACK - 1)].indirect(offsets[:]), COPY)
         iw0(0, S)
         gather(1, 3, 0, S)
         gather(1, 0, 0, S)
@@ -168,28 +172,30 @@ def tile_picked_neuron_lin_bias_srt_e_kernel(tc, w, xT, b, offs, out):
         qw(0, 0, S)
         gather(1, 1, 0, S)
         gather(1, 2, 0, HALF)
+        last_half = keep.tile([P, HALF], BF16, name="last_half", align_bytes=ALIGN)
+        nc.scalar.activation(last_half[:], w_slot[(1, 2)].indirect(offsets[:, HALF // OFFS_PER_COLUMN :]), COPY)
         ixs(0, 0)
+        ixs(1, 0)
         ixs(0, 1)
-        gather(1, 2, HALF, S)
+        nc.vector.tensor_copy(w_grp[1][:, HALF:S, 2], last_half[:])
         qx(0, 0)
         mm(0, 0, range(4))
         open_w_codes(1, 0, HALF, "x_grp0_0")
         qw(1, 0, HALF)
+        qx(1, 0)
+        open_w_codes(1, HALF, S, "x_grp1_0")
+        qw(1, HALF, S)
+        mm(1, 0, range(4))
+        ixv(1, 1)
         qx(0, 1)
         mm(0, 1, range(4))
-        open_w_codes(1, HALF, S, "x_grp0_1")
-        qw(1, HALF, S)
-        ixs(1, 0)
-        ixs(1, 1)
-        qx(1, 0)
-        mm(1, 0, range(4))
-        ixv(0, 2)
         qx(1, 1)
         mm(1, 1, range(4))
-        open_result(0, (1, 1))
+        open_result(0, (0, 1))
         for m in range(BLOCKS):
             evs(0, m)
         store(0, 0, 4)
+        ixv(0, 2)
         ixv(1, 2)
         qx(0, 2)
         mm(0, 2, range(4))

@@ -21,6 +21,7 @@ PASSES = K // K_PASS
 BLOCKS = S // P
 OFFS_PER_COLUMN = 16
 ALIGN = 256
+SCALAR_SHARE = 192
 CHUNKS = [(0, 128), (128, 256), (256, 384), (384, 448), (448, 512)]
 
 
@@ -42,7 +43,21 @@ def tile_picked_neuron_lin_bias_srt_e_kernel(tc, w, xT, b, offs, out):
             for j in range(PACK)
         }
         x_raw = {(a, c): keep.tile([P, PACK, width[c]], F32, name="x_raw%d_%d" % (a, c), tag="x_raw%d_%d" % (a, c), align_bytes=ALIGN) for a, c in pieces}
-        x_grp = {(a, c): keep.tile([P, width[c], PACK], BF16, name="x_grp%d_%d" % (a, c), tag="x_grp%d_%d" % (a, c), align_bytes=ALIGN) for a, c in pieces}
+        x_grp = {(a, c): keep.tile([P, width[c], PACK], BF16, name="x_grp%d_%d" % (a, c), tag="x_grp%d_%d" % (a, c), align_bytes=ALIGN)[:] for a, c in pieces[:5]}
+        x_late = keep.tile([P, 3 * P, PACK], BF16, name="x_late", align_bytes=ALIGN)
+        x_grp[(1, 2)] = x_late[:, 0:P, :]
+        for i, pc in enumerate(pieces[6:]):
+            x_grp[pc] = x_late[:, P + 64 * i : P + 64 * (i + 1), :]
+        window = {}
+
+        def quantize_window(pc, columns, after):
+            i = pieces[6:].index(pc)
+            codes = keep.tile([P, columns], U32, name="window_codes%d" % i, tag="x_raw%d_%d" % after, align_bytes=ALIGN)
+            scales = keep.tile([P, columns], U8, name="window_scales%d" % i, align_bytes=ALIGN)
+            quantize(codes[:, 0:P], scales[:, 0:P], x_late[:, 64 * (i + 1) : 64 * (i + 1) + P, :])
+            window[pc] = (codes[:, 0:P], scales[:, 0:P])
+            return codes, scales
+
         x_codes = [keep.tile([P, T], U32, name="x_codes%d" % a, align_bytes=ALIGN) for a in range(PASSES)]
         x_scales = [keep.tile([P, T], U8, name="x_scales%d" % a, align_bytes=ALIGN) for a in range(PASSES)]
         w_grp = [keep.tile([P, S, PACK], BF16, name="w_grp%d" % a, align_bytes=ALIGN) for a in range(PASSES)]
@@ -118,7 +133,8 @@ def tile_picked_neuron_lin_bias_srt_e_kernel(tc, w, xT, b, offs, out):
 
         def qx(a, c):
             lo, hi = CHUNKS[c]
-            quantize(x_codes[a][:, lo:hi], x_scales[a][:, lo:hi], x_grp[(a, c)][:])
+            quantize(x_codes[a][:, lo:hi], x_scales[a][:, lo:hi], x_grp[(a, c)])
+            window[(a, c)] = (x_codes[a][:, lo:hi], x_scales[a][:, lo:hi])
 
         def ixs(a, c, lo=0, hi=None):
             hi = width[c] if hi is None else hi
@@ -143,8 +159,8 @@ def tile_picked_neuron_lin_bias_srt_e_kernel(tc, w, xT, b, offs, out):
                     out=acc(c, m),
                     lhsT=w_codes[(a, m)].bitcast(FP8X4),
                     lhsT_scale=w_scales[a][:, cols],
-                    rhs=x_codes[a][:, CHUNKS[c][1] - P : CHUNKS[c][1]].bitcast(FP8X4),
-                    rhs_scale=x_scales[a][:, CHUNKS[c][1] - P : CHUNKS[c][1]],
+                    rhs=window[(a, c)][0].bitcast(FP8X4),
+                    rhs_scale=window[(a, c)][1],
                     start=(a == first),
                     stop=(a != first),
                 )
@@ -171,16 +187,16 @@ def tile_picked_neuron_lin_bias_srt_e_kernel(tc, w, xT, b, offs, out):
         open_w_codes(0, 0, S, "w_codes0")
         qw(0, 0, S)
         gather(1, 1, 0, S)
-        gather(1, 2, 0, HALF)
-        last_half = keep.tile([P, HALF], BF16, name="last_half", align_bytes=ALIGN)
-        nc.scalar.activation(last_half[:], w_slot[(1, 2)].indirect(offsets[:, HALF // OFFS_PER_COLUMN :]), COPY)
+        gather(1, 2, 0, S - SCALAR_SHARE)
+        last_share = keep.tile([P, SCALAR_SHARE], BF16, name="last_share", align_bytes=ALIGN)
+        nc.scalar.activation(last_share[:], w_slot[(1, 2)].indirect(offsets[:, (S - SCALAR_SHARE) // OFFS_PER_COLUMN :]), COPY)
         ixs(0, 0)
         ixs(1, 0)
         ixs(0, 1)
-        nc.vector.tensor_copy(w_grp[1][:, HALF:S, 2], last_half[:])
+        nc.vector.tensor_copy(w_grp[1][:, S - SCALAR_SHARE : S, 2], last_share[:])
         qx(0, 0)
         mm(0, 0, range(4))
-        open_w_codes(1, 0, HALF, "x_grp0_0")
+        open_w_codes(1, 0, HALF, "x_raw0_0")
         qw(1, 0, HALF)
         qx(1, 0)
         open_w_codes(1, HALF, S, "x_grp1_0")
@@ -207,10 +223,10 @@ def tile_picked_neuron_lin_bias_srt_e_kernel(tc, w, xT, b, offs, out):
             evs(1, m)
         store(1, 0, 4)
         ixv(1, 3)
-        qx(0, 3)
+        first_codes, first_scales = quantize_window((0, 3), P + 64, (1, 3))
         mm(0, 3, range(4))
         ixv(0, 4)
-        qx(1, 3)
+        last_codes, last_scales = quantize_window((1, 3), P + 64, (0, 4))
         mm(1, 3, range(4))
         open_result(2)
         for m in range(BLOCKS):
@@ -218,9 +234,11 @@ def tile_picked_neuron_lin_bias_srt_e_kernel(tc, w, xT, b, offs, out):
             if m % 2 == 1:
                 store(2, m - 1, m + 1)
         ixv(1, 4)
-        qx(0, 4)
+        quantize(first_codes[:, P : P + 64], first_scales[:, P : P + 64], x_grp[(0, 4)])
+        window[(0, 4)] = (first_codes[:, 64 : P + 64], first_scales[:, 64 : P + 64])
         mm(0, 4, range(4))
-        qx(1, 4)
+        quantize(last_codes[:, P : P + 64], last_scales[:, P : P + 64], x_grp[(1, 4)])
+        window[(1, 4)] = (last_codes[:, 64 : P + 64], last_scales[:, 64 : P + 64])
         mm(1, 4, range(4))
         open_result(3)
         for m in range(BLOCKS):

@@ -34,14 +34,15 @@ def tile_picked_neuron_lin_bias_srt_e_kernel(tc, w, xT, b, offs, out):
         pieces = [(a, c) for c in range(len(CHUNKS)) for a in range(PASSES)]
         width = [hi - lo for lo, hi in CHUNKS]
         offsets = keep.tile([P, S // OFFS_PER_COLUMN], U16, name="offsets", align_bytes=ALIGN)
-        w_first = keep.tile([P, PACK - 1, N], F32, name="w_first", align_bytes=ALIGN)
-        w_last_slots = keep.tile([P, PASSES, N], F32, name="w_last_slots", align_bytes=ALIGN)
-        w_single = [keep.tile([P, N], F32, name="w_single%d" % j, align_bytes=ALIGN) for j in range(PACK - 1)]
-        w_slot = {
-            (a, j): w_last_slots[:, a, :] if j == PACK - 1 else (w_first[:, j, :] if a == 0 else w_single[j][:])
-            for a in range(PASSES)
-            for j in range(PACK)
-        }
+        w_first = keep.tile([P, PACK, N], F32, name="w_first", align_bytes=ALIGN)
+        w_pair = keep.tile([P, 2, N], F32, name="w_pair", align_bytes=ALIGN)
+        w_single = [keep.tile([P, N], F32, name="w_single%d" % j, align_bytes=ALIGN) for j in range(2)]
+        pair_planes = keep.tile([P, 2, S], F32, name="pair_planes", align_bytes=ALIGN)
+        w_slot = {(0, j): w_first[:, j, :] for j in range(PACK)}
+        w_slot[(1, 0)] = w_single[0][:]
+        w_slot[(1, 1)] = w_single[1][:]
+        w_slot[(1, 2)] = w_pair[:, 0, :]
+        w_slot[(1, 3)] = w_pair[:, 1, :]
         x_raw = {(a, c): keep.tile([P, PACK, width[c]], F32, name="x_raw%d_%d" % (a, c), tag="x_raw%d_%d" % (a, c), align_bytes=ALIGN) for a, c in pieces}
         x_grp = {(a, c): keep.tile([P, width[c], PACK], BF16, name="x_grp%d_%d" % (a, c), tag="x_grp%d_%d" % (a, c), align_bytes=ALIGN)[:] for a, c in pieces[:5]}
         x_late = keep.tile([P, 3 * P, PACK], BF16, name="x_late", align_bytes=ALIGN)
@@ -89,11 +90,11 @@ def tile_picked_neuron_lin_bias_srt_e_kernel(tc, w, xT, b, offs, out):
         def load_offs():
             nc.sync.dma_start(offsets[:], offs)
 
-        nc.sync.dma_start(out=w_first[:], in_=w_view[0][:, 0 : PACK - 1, :])
+        nc.sync.dma_start(out=w_first[:], in_=w_view[0])
         load_offs()
         load_bias()
-        nc.sync.dma_start(out=w_last_slots[:], in_=w.rearrange("(a p j) n -> p a j n", p=P, j=PACK)[:, :, PACK - 1, :])
-        for j in range(PACK - 1):
+        nc.sync.dma_start(out=w_pair[:], in_=w_view[1][:, 2:4, :])
+        for j in range(2):
             nc.sync.dma_start(out=w_single[j][:], in_=w_view[1][:, j, :])
         for a, c in pieces:
             load_x(a, c)
@@ -178,22 +179,24 @@ def tile_picked_neuron_lin_bias_srt_e_kernel(tc, w, xT, b, offs, out):
         def store(c, m0, m1, queue=nc.sync):
             queue.dma_start(out=out_view[:, m0:m1, CHUNKS[c][0] : CHUNKS[c][1]], in_=result[c][:, m0:m1, :])
 
-        for j in range(PACK - 1):
+        for j in range(2):
             gather0(j)
-        nc.scalar.activation(g4[:, PACK - 1, :], w_slot[(0, PACK - 1)].indirect(offsets[:]), COPY)
-        iw0(0, S)
-        gather(1, 3, 0, S)
-        gather(1, 0, 0, S)
+            nc.scalar.activation(g4[:, 2 + j, :], w_slot[(0, 2 + j)].indirect(offsets[:]), COPY)
+        nc.vector.tensor_copy(*by_fours(w_grp[0][:, 0:HALF, :], g4[:, :, 0:HALF]))
+        iw0(HALF, S)
         open_w_codes(0, 0, S, "w_codes0")
         qw(0, 0, S)
-        gather(1, 1, 0, S)
-        gather(1, 2, 0, S - SCALAR_SHARE)
+        nc.vector.tensor_copy(pair_planes[:, 0, :], w_slot[(1, 2)].indirect(offsets[:]))
+        nc.scalar.activation(pair_planes[:, 1, :], w_slot[(1, 3)].indirect(offsets[:]), COPY)
+        nc.vector.tensor_copy(w_grp[1][:, :, 2:4], pair_planes[:].rearrange("p j s -> p s j"))
+        gather(1, 0, 0, S)
+        gather(1, 1, 0, S - SCALAR_SHARE)
         last_share = keep.tile([P, SCALAR_SHARE], BF16, name="last_share", align_bytes=ALIGN)
-        nc.scalar.activation(last_share[:], w_slot[(1, 2)].indirect(offsets[:, (S - SCALAR_SHARE) // OFFS_PER_COLUMN :]), COPY)
+        nc.scalar.activation(last_share[:], w_slot[(1, 1)].indirect(offsets[:, (S - SCALAR_SHARE) // OFFS_PER_COLUMN :]), COPY)
         ixs(0, 0)
         ixs(1, 0)
         ixs(0, 1)
-        nc.vector.tensor_copy(w_grp[1][:, S - SCALAR_SHARE : S, 2], last_share[:])
+        nc.vector.tensor_copy(w_grp[1][:, S - SCALAR_SHARE : S, 1], last_share[:])
         qx(0, 0)
         mm(0, 0, range(4))
         open_w_codes(1, 0, HALF, "x_raw0_0")

@@ -224,7 +224,8 @@ def tile_picked_neuron_lin_bias_srt_e_kernel(tc, w, xT, b, offs, out):
         open_result(1)
         for m in range(BLOCKS):
             evs(1, m)
-        store(1, 0, 4)
+            if m % 2 == 1:
+                store(1, m - 1, m + 1)
         ixv(1, 3)
         first_codes, first_scales = quantize_window((0, 3), P + 64, (1, 3))
         mm(0, 3, range(4))

@@ -250,5 +250,5 @@ def tile_picked_neuron_lin_bias_srt_e_kernel(tc, w, xT, b, offs, out):
         store(3, 0, 4)
         open_result(4)
         for m in range(BLOCKS):
-            (evs if m % 2 == 1 else evv)(4, m)
+            evv(4, m)
         store(4, 0, 4)

from contextlib import ExitStack

import concourse.mybir as mybir

K, N, S, T = 1024, 2048, 512, 512
FLOPS = 2 * K * S * T

F32 = mybir.dt.float32
BF16 = mybir.dt.bfloat16
U32 = mybir.dt.uint32
U16 = mybir.dt.uint16
U8 = mybir.dt.uint8
FP8X4 = mybir.dt.float8_e4m3fn_x4
IDENTITY = mybir.ActivationFunctionType.Identity
COPY = mybir.ActivationFunctionType.Copy

P = 128
PACK = 4
K_PASS = P * PACK
PASSES = K // K_PASS
BLOCKS = S // P
OFFS_PER_COLUMN = 16
ALIGN = 256
SCALAR_SHARE = 192
CHUNKS = [(0, 128), (128, 256), (256, 384), (384, 448), (448, 512)]


def tile_picked_neuron_lin_bias_srt_e_kernel(tc, w, xT, b, offs, out):
    nc = tc.nc
    with ExitStack() as ctx:
        keep = ctx.enter_context(tc.tile_pool(name="keep", bufs=1))
        psum = ctx.enter_context(tc.psum_pool(name="psum", bufs=1))

        pieces = [(a, c) for c in range(len(CHUNKS)) for a in range(PASSES)]
        width = [hi - lo for lo, hi in CHUNKS]
        offsets = keep.tile([P, S // OFFS_PER_COLUMN], U16, name="offsets", align_bytes=ALIGN)
        w_first = keep.tile([P, PACK, N], F32, name="w_first", align_bytes=ALIGN)
        w_pair = keep.tile([P, 2, N], F32, name="w_pair", align_bytes=ALIGN)
        w_single = [keep.tile([P, N], F32, name="w_single%d" % j, align_bytes=ALIGN) for j in range(2)]
        pair_planes = keep.tile([P, 2, S], F32, name="pair_planes", align_bytes=ALIGN)
        w_slot = {(0, j): w_first[:, j, :] for j in range(PACK)}
        w_slot[(1, 0)] = w_single[0][:]
        w_slot[(1, 1)] = w_single[1][:]
        w_slot[(1, 2)] = w_pair[:, 0, :]
        w_slot[(1, 3)] = w_pair[:, 1, :]
        x_raw = {(a, c): keep.tile([P, PACK, width[c]], F32, name="x_raw%d_%d" % (a, c), tag="x_raw%d_%d" % (a, c), align_bytes=ALIGN) for a, c in pieces}
        x_grp = {(a, c): keep.tile([P, width[c], PACK], BF16, name="x_grp%d_%d" % (a, c), tag="x_grp%d_%d" % (a, c), align_bytes=ALIGN)[:] for a, c in pieces[:5]}
        x_late = keep.tile([P, 3 * P, PACK], BF16, name="x_late", align_bytes=ALIGN)
        x_grp[(1, 2)] = x_late[:, 0:P, :]
        for i, pc in enumerate(pieces[6:]):
            x_grp[pc] = x_late[:, P + 64 * i : P + 64 * (i + 1), :]
        window = {}

        def quantize_window(pc, columns, after):
            i = pieces[6:].index(pc)
            codes = keep.tile([P, columns], U32, name="window_codes%d" % i, tag="x_raw%d_%d" % after, align_bytes=ALIGN)
            scales = keep.tile([P, columns], U8, name="window_scales%d" % i, align_bytes=ALIGN)
            quantize(codes[:, 0:P], scales[:, 0:P], x_late[:, 64 * (i + 1) : 64 * (i + 1) + P, :])
            window[pc] = (codes[:, 0:P], scales[:, 0:P])
            return codes, scales

        x_codes = [keep.tile([P, T], U32, name="x_codes%d" % a, align_bytes=ALIGN) for a in range(PASSES)]
        x_scales = [keep.tile([P, T], U8, name="x_scales%d" % a, align_bytes=ALIGN) for a in range(PASSES)]
        w_grp = [keep.tile([P, S, PACK], BF16, name="w_grp%d" % a, align_bytes=ALIGN) for a in range(PASSES)]
        g4 = keep.tile([P, PACK, S], F32, name="g4", align_bytes=ALIGN)
        HALF = S // 2
        w_codes = {}
        w_scales = [keep.tile([P, S], U8, name="w_scales%d" % a, align_bytes=ALIGN) for a in range(PASSES)]
        result = {}
        b_rows = keep.tile([P, BLOCKS * 32], F32, name="b_rows", align_bytes=ALIGN)
        b_cols = keep.tile([P, BLOCKS * 32], F32, name="b_cols", align_bytes=ALIGN)

        w_view = [w[a * K_PASS : (a + 1) * K_PASS, :].rearrange("(p j) n -> p j n", j=PACK) for a in range(PASSES)]
        x_view = [xT[a * K_PASS : (a + 1) * K_PASS, :].rearrange("(p j) t -> p j t", j=PACK) for a in range(PASSES)]
        out_view = out.rearrange("(m p) t -> p m t", p=P)

        def load_x(a, c, queue=nc.sync):
            queue.dma_start(out=x_raw[(a, c)][:], in_=x_view[a][:, :, CHUNKS[c][0] : CHUNKS[c][1]])

        def load_bias():
            zero = keep.tile([P, 1], F32, name="zero", align_bytes=ALIGN)
            nc.vector.memset(zero[:], 0.0)
            nc.scalar.activation(b_rows[:], zero[:].to_broadcast([P, BLOCKS * 32]), COPY)
            nc.sync.dma_start(
                out=b_rows[0:P:32, :].rearrange("q (m c) -> q m c", c=32),
                in_=b.rearrange("(m q c) o -> q m (c o)", m=BLOCKS, c=32),
            )
            nc.vector.transpose(b_cols[:], b_rows[:])

        def load_offs():
            nc.sync.dma_start(offsets[:], offs)

        nc.sync.dma_start(out=w_first[:], in_=w_view[0])
        load_offs()
        load_bias()
        nc.sync.dma_start(out=w_pair[:], in_=w_view[1][:, 2:4, :])
        for j in range(2):
            nc.sync.dma_start(out=w_single[j][:], in_=w_view[1][:, j, :])
        for a, c in pieces:
            load_x(a, c)

        banks = [psum.tile([P, 512], F32, name="bank%d" % i) for i in range(8)]

        def gather(a, j, lo, hi):
            nc.vector.tensor_copy(
                w_grp[a][:, lo:hi, j],
                w_slot[(a, j)].indirect(offsets[:, lo // OFFS_PER_COLUMN : hi // OFFS_PER_COLUMN]),
            )

        def gather0(j):
            nc.vector.tensor_copy(g4[:, j, :], w_slot[(0, j)].indirect(offsets[:]))

        def by_fours(grouped, raw):
            return (
                grouped.rearrange("p (c i) j -> p c j i", i=4),
                raw.rearrange("p j (c i) -> p c j i", i=4),
            )

        def iw0(lo, hi):
            dst, src = by_fours(w_grp[0][:, lo:hi, :], g4[:, :, lo:hi])
            nc.scalar.copy(dst, src)

        def quantize(codes, scales, grp):
            nc.vector.quantize_mx(out=codes.bitcast(FP8X4), scales=scales, in_=grp.rearrange("p s j -> p (s j)"))

        def open_w_codes(a, lo, hi, tag):
            t = keep.tile([P, hi - lo], U32, name="w_codes%d_%d" % (a, lo), tag=tag, align_bytes=ALIGN)
            for m in range(lo // P, hi // P):
                w_codes[(a, m)] = t[:, m * P - lo : (m + 1) * P - lo]
            w_codes[(a, lo, hi)] = t

        def qw(a, lo, hi):
            quantize(w_codes[(a, lo, hi)][:], w_scales[a][:, lo:hi], w_grp[a][:, lo:hi, :])

        def qx(a, c):
            lo, hi = CHUNKS[c]
            quantize(x_codes[a][:, lo:hi], x_scales[a][:, lo:hi], x_grp[(a, c)])
            window[(a, c)] = (x_codes[a][:, lo:hi], x_scales[a][:, lo:hi])

        def ixs(a, c, lo=0, hi=None):
            hi = width[c] if hi is None else hi
            dst, src = by_fours(x_grp[(a, c)][:, lo:hi, :], x_raw[(a, c)][:, :, lo:hi])
            nc.scalar.copy(dst, src)

        def ixv(a, c, lo=0, hi=None):
            hi = width[c] if hi is None else hi
            dst, src = by_fours(x_grp[(a, c)][:, lo:hi, :], x_raw[(a, c)][:, :, lo:hi])
            nc.vector.tensor_copy(dst, src)

        def acc(c, m):
            return banks[4 * (c % 2) + m][:, (c // 2) * P : (c // 2 + 1) * P]

        def acc_real(c, m):
            return acc(c, m)[:, P - width[c] : P]

        def mm(a, c, ms, first=0):
            for m in ms:
                cols = slice(m * P, (m + 1) * P)
                nc.tensor.matmul_mx(
                    out=acc(c, m),
                    lhsT=w_codes[(a, m)].bitcast(FP8X4),
                    lhsT_scale=w_scales[a][:, cols],
                    rhs=window[(a, c)][0].bitcast(FP8X4),
                    rhs_scale=window[(a, c)][1],
                    start=(a == first),
                    stop=(a != first),
                )

        def open_result(c, after=None):
            tag = "result%d" % c if after is None else "x_raw%d_%d" % after
            result[c] = keep.tile([P, BLOCKS, width[c]], F32, name="result%d" % c, tag=tag, align_bytes=ALIGN)

        def evs(c, m):
            nc.scalar.activation(result[c][:, m, :], acc_real(c, m), IDENTITY, bias=b_cols[:, 32 * m : 32 * m + 1])

        def evv(c, m):
            nc.vector.tensor_scalar_add(result[c][:, m, :], acc_real(c, m), b_cols[:, 32 * m : 32 * m + 1])

        def store(c, m0, m1, queue=nc.sync):
            queue.dma_start(out=out_view[:, m0:m1, CHUNKS[c][0] : CHUNKS[c][1]], in_=result[c][:, m0:m1, :])

        for j in range(2):
            gather0(j)
            nc.scalar.activation(g4[:, 2 + j, :], w_slot[(0, 2 + j)].indirect(offsets[:]), COPY)
        nc.vector.tensor_copy(*by_fours(w_grp[0][:, 0:HALF, :], g4[:, :, 0:HALF]))
        iw0(HALF, S)
        open_w_codes(0, 0, S, "w_codes0")
        qw(0, 0, S)
        nc.vector.tensor_copy(pair_planes[:, 0, :], w_slot[(1, 2)].indirect(offsets[:]))
        nc.scalar.activation(pair_planes[:, 1, :], w_slot[(1, 3)].indirect(offsets[:]), COPY)
        nc.vector.tensor_copy(w_grp[1][:, :, 2:4], pair_planes[:].rearrange("p j s -> p s j"))
        gather(1, 0, 0, S)
        gather(1, 1, 0, S - SCALAR_SHARE)
        last_share = keep.tile([P, SCALAR_SHARE], BF16, name="last_share", align_bytes=ALIGN)
        nc.scalar.activation(last_share[:], w_slot[(1, 1)].indirect(offsets[:, (S - SCALAR_SHARE) // OFFS_PER_COLUMN :]), COPY)
        ixs(0, 0)
        ixs(1, 0)
        ixs(0, 1)
        nc.vector.tensor_copy(w_grp[1][:, S - SCALAR_SHARE : S, 1], last_share[:])
        qx(0, 0)
        mm(0, 0, range(4))
        open_w_codes(1, 0, HALF, "x_raw0_0")
        qw(1, 0, HALF)
        qx(1, 0)
        open_w_codes(1, HALF, S, "x_grp1_0")
        qw(1, HALF, S)
        mm(1, 0, range(4))
        ixv(1, 1)
        qx(0, 1)
        mm(0, 1, range(4))
        qx(1, 1)
        mm(1, 1, range(4))
        open_result(0, (0, 1))
        for m in range(BLOCKS):
            evs(0, m)
        store(0, 0, 4)
        ixv(0, 2)
        ixv(1, 2)
        qx(0, 2)
        mm(0, 2, range(4))
        ixv(0, 3)
        qx(1, 2)
        mm(1, 2, range(4))
        open_result(1)
        for m in range(BLOCKS):
            evs(1, m)
            if m % 2 == 1:
                store(1, m - 1, m + 1)
        ixv(1, 3)
        first_codes, first_scales = quantize_window((0, 3), P + 64, (1, 3))
        mm(0, 3, range(4))
        ixv(0, 4)
        last_codes, last_scales = quantize_window((1, 3), P + 64, (0, 4))
        mm(1, 3, range(4))
        open_result(2)
        for m in range(BLOCKS):
            evs(2, m)
            if m % 2 == 1:
                store(2, m - 1, m + 1)
        ixv(1, 4)
        quantize(first_codes[:, P : P + 64], first_scales[:, P : P + 64], x_grp[(0, 4)])
        window[(0, 4)] = (first_codes[:, 64 : P + 64], first_scales[:, 64 : P + 64])
        mm(0, 4, range(4))
        quantize(last_codes[:, P : P + 64], last_scales[:, P : P + 64], x_grp[(1, 4)])
        window[(1, 4)] = (last_codes[:, 64 : P + 64], last_scales[:, 64 : P + 64])
        mm(1, 4, range(4))
        open_result(3)
        for m in range(BLOCKS):
            evs(3, m)
        store(3, 0, 4)
        open_result(4)
        for m in range(BLOCKS):
            evv(4, m)
        store(4, 0, 4)
